import numpy as np
import ml_dtypes


def mxq(x, axis, fmt="e4m3"):
    dtype, down = {"e4m3": (ml_dtypes.float8_e4m3fn, 7), "e5m2": (ml_dtypes.float8_e5m2, 14)}[fmt]
    v = np.moveaxis(np.asarray(x, np.float32).astype(ml_dtypes.bfloat16).astype(np.float64), axis, -1)
    blocks = v.reshape(v.shape[:-1] + (-1, 32))
    amax = np.abs(blocks).max(-1, keepdims=True)
    byte = np.maximum(np.where(amax > 0, np.frexp(amax)[1] - 1 + 127, 0) - down, 1)
    scale = np.exp2(byte - 127.0)
    codes = (blocks / scale).astype(np.float32).astype(dtype).astype(np.float64)
    return np.moveaxis((codes * scale).reshape(v.shape), -1, axis)


WIDE = False


def mx_kscale(k):
    if not WIDE:
        return np.ones(k)
    levels = np.array([10, -10, 5, -5, 0])
    if k % 512:
        return np.exp2(np.random.permutation(np.resize(levels, k // 32))).repeat(32)
    a = np.empty((k // 512, 16))
    for p in range(k // 512):
        a[p, :8] = np.random.permutation(np.resize(levels, 8))
        for g in range(8):
            far = levels[np.abs(levels - a[p, g]) >= 10]
            a[p, g + 8] = far[np.random.randint(len(far))]
    return np.exp2(a.ravel()).repeat(32)


def f64(x):
    return np.asarray(x).astype(np.float64)


def striped8(idx):
    return np.asarray(idx).reshape(8, -1, 16).transpose(0, 2, 1).reshape(128, -1).astype(np.uint16)


def unstriped8(offs):
    return offs.reshape(8, 16, -1).transpose(0, 2, 1).reshape(8, -1).astype(np.int64)


def pick8(x, idx, run):
    r = np.arange(len(x))
    return x[r[:, None], idx[r % (8 * run) // run]]


E2M1 = np.array([0.0, 0.5, 1.0, 1.5, 2.0, 3.0, 4.0, 6.0, -0.0, -0.5, -1.0, -1.5, -2.0, -3.0, -4.0, -6.0])


def pack_weight(w, fmt):
    k, n = w.shape
    w = f64(np.asarray(w, np.float32).astype(ml_dtypes.bfloat16)).reshape(k // 32, 32, n)
    amax = np.abs(w).max(1)
    if fmt == "e4m3":
        byte = np.frexp(amax)[1] - 1 + 127 - 7
    else:
        mant, ex = np.frexp(amax / 6.0)
        byte = np.where(mant > 0.5, ex, ex - 1) + 127
    byte = np.clip(np.where(amax > 0, byte, 1), 1, 254)
    scaled = (w * np.exp2(127.0 - byte)[:, None, :]).reshape(k, n).astype(np.float32)
    by_word = np.ascontiguousarray(scaled.reshape(k // 512, 128, 4, n).transpose(0, 1, 3, 2))
    if fmt == "e4m3":
        words = by_word.astype(ml_dtypes.float8_e4m3fn).view(np.uint8)
    else:
        c = by_word.astype(ml_dtypes.float4_e2m1fn).view(np.uint8) & 0xF
        words = (c[..., 0::2] | (c[..., 1::2] << 4)).reshape(k // 512, 128, 2 * n)
    return np.ascontiguousarray(words), np.ascontiguousarray(byte.astype(np.uint8).reshape(k // 512, 16, n))


def unpack_weight(words, scales, fmt):
    g, _, n = scales.shape
    words = np.ascontiguousarray(words).reshape(g, 128, n, -1)
    if fmt == "e4m3":
        vals = words.view(ml_dtypes.float8_e4m3fn).astype(np.float64)
    else:
        nib = np.empty((g, 128, n, 4), np.uint8)
        nib[..., 0::2] = words & 0xF
        nib[..., 1::2] = words >> 4
        vals = E2M1[nib]
    vals = vals * np.repeat(np.exp2(scales.astype(np.float64) - 127.0), 8, axis=1)[..., None]
    return vals.transpose(0, 1, 3, 2).reshape(g * 512, n)


D, T, U, X, I, Q = 512, 1024, 1024, 1024, 512, 128


def setup_inputs():
    n = np.random.standard_normal
    idx = np.stack([np.random.permutation(T)[:I] for _ in range(8)])
    idx2 = np.stack([np.random.permutation(U)[:I] for _ in range(8)])
    idx3 = np.stack([np.random.permutation(X)[:I] for _ in range(8)])
    idx4 = np.stack([np.random.permutation(X)[:I] for _ in range(8)])
    idx5 = np.stack([np.random.permutation(U)[:I] for _ in range(8)])
    idx6 = np.stack([np.random.permutation(T)[:I] for _ in range(8)])
    fd = mx_kscale(D)
    keysp = pack_weight(n((D, T)) / fd[:, None], "e2m1")
    notesp = pack_weight(n((D, U)) / fd[:, None], "e4m3")
    usersp = pack_weight(n((D, X)) / fd[:, None], "e2m1")
    return {
        "query": (n((D, Q)) * 1.0 / np.sqrt(D) * fd[:, None]).astype(np.float32),
        "keys_words": keysp[0],
        "keys_scales": keysp[1],
        "notes_words": notesp[0],
        "notes_scales": notesp[1],
        "users_words": usersp[0],
        "users_scales": usersp[1],
        "lam": (np.random.uniform(0.5, 1.2, (Q, 1))).astype(np.float32),
        "offs": striped8(idx),
        "offs2": striped8(idx2),
        "offs3": striped8(idx3),
        "offs4": striped8(idx4),
        "offs5": striped8(idx5),
        "offs6": striped8(idx6),
    }


def reference(query, keys_words, keys_scales, notes_words, notes_scales, users_words, users_scales, lam, offs, offs2, offs3, offs4, offs5, offs6):
    idx = unstriped8(offs)
    idx2 = unstriped8(offs2)
    idx3 = unstriped8(offs3)
    idx4 = unstriped8(offs4)
    idx5 = unstriped8(offs5)
    idx6 = unstriped8(offs6)
    keysu = unpack_weight(keys_words, keys_scales, "e2m1")
    notesu = unpack_weight(notes_words, notes_scales, "e4m3")
    usersu = unpack_weight(users_words, users_scales, "e2m1")
    queryq = mxq(f64(query), 0, "e4m3")
    a = queryq.T @ keysu
    b = queryq.T @ notesu
    c0 = queryq.T @ usersu
    w = np.maximum(pick8(b, idx2, 16), pick8(c0, idx3, 16))
    f1 = np.zeros((Q, X))
    f1[np.arange(Q)[:, None], idx4[np.arange(Q) % 128 // 16]] = pick8(a, idx, 16)
    cc = c0 + f1
    v = pick8(cc, idx3, 16) - w
    f2 = np.zeros((Q, U))
    f2[np.arange(Q)[:, None], idx5[np.arange(Q) % 128 // 16]] = v
    bb = b + f2 * f64(lam)
    y = np.minimum(pick8(bb, idx2, 16), pick8(a, idx6, 16))
    return y

@@ -1,0 +1,170 @@
+from contextlib import ExitStack
+
+import concourse.mybir as mybir
+
+F32 = mybir.dt.float32
+BF16 = mybir.dt.bfloat16
+I32 = mybir.dt.int32
+U32 = mybir.dt.uint32
+U16 = mybir.dt.uint16
+U8 = mybir.dt.uint8
+FP8X4 = mybir.dt.float8_e4m3fn_x4
+FP4X4 = mybir.dt.float4_e2m1fn_x4
+ALU = mybir.AluOpType
+COPY = mybir.ActivationFunctionType.Copy
+
+P = 128
+PACK = 4
+Q = 128
+POOL = 1024
+SLOTS = 512
+HALF = SLOTS // 2
+BANK = 512
+PIECE = 256
+LIST_COLS = SLOTS // 16
+FLOPS = 2 * 512 * Q * 3 * POOL
+
+
+def load_scales(queue, plane, scales):
+    for quad in range(4):
+        queue.dma_start(
+            out=plane[32 * quad : 32 * quad + 4, :].bitcast(I32),
+            in_=scales[0, 4 * quad : 4 * quad + 4, :].bitcast(I32),
+        )
+
+
+def tile_attend_goaround_three_kernel(
+    tc, query, keys_words, keys_scales, notes_words, notes_scales, users_words, users_scales,
+    lam, offs, offs2, offs3, offs4, offs5, offs6, out,
+):
+    nc = tc.nc
+    with ExitStack() as ctx:
+        lists = ctx.enter_context(tc.tile_pool(name="lists", bufs=1))
+        sb = ctx.enter_context(tc.tile_pool(name="sb", bufs=1))
+        psum = ctx.enter_context(tc.psum_pool(name="psum", bufs=1))
+
+        def load_list(source, name):
+            held = lists.tile([P, LIST_COLS], U16, name=name)
+            nc.sync.dma_start(held[:], source)
+            return held
+
+        def half(held, h):
+            return held[:, h * (LIST_COLS // 2) : (h + 1) * (LIST_COLS // 2)]
+
+        def slots(values, h):
+            return values[:, h * HALF : (h + 1) * HALF]
+
+        keys_plane = sb.tile([P, POOL], U8, align_bytes=64)
+        users_plane = sb.tile([P, POOL], U8, align_bytes=64)
+        notes_plane = sb.tile([P, POOL], U8, align_bytes=64)
+        f1 = sb.tile([P, POOL], F32)
+        f2 = sb.tile([P, POOL], F32)
+        nc.vector.memset(keys_plane[:].bitcast(I32), 0)
+        nc.vector.memset(users_plane[:].bitcast(I32), 0)
+        nc.vector.memset(notes_plane[:].bitcast(I32), 0)
+        nc.vector.memset(f1[:], 0.0)
+        nc.vector.memset(f2[:], 0.0)
+
+        query_rows = sb.tile([P, PACK, Q], F32)
+        nc.sync.dma_start(out=query_rows[:], in_=query.rearrange("(p j) q -> p j q", j=PACK))
+        keys_codes = sb.tile([P, 2 * POOL], U8, align_bytes=64)
+        nc.sync.dma_start(out=keys_codes[:].bitcast(I32), in_=keys_words[0].bitcast(I32))
+        load_scales(nc.scalar, keys_plane, keys_scales)
+        idx = load_list(offs, "idx")
+        idx4 = load_list(offs4, "idx4")
+        users_codes = sb.tile([P, 2 * POOL], U8, align_bytes=64)
+        nc.sync.dma_start(out=users_codes[:].bitcast(I32), in_=users_words[0].bitcast(I32))
+        load_scales(nc.sync, users_plane, users_scales)
+        notes_codes = sb.tile([P, POOL], U32, align_bytes=64)
+        nc.sync.dma_start(
+            out=notes_codes[:].bitcast(I32), in_=notes_words[0].rearrange("p n t -> p (n t)").bitcast(I32)
+        )
+        load_scales(nc.sync, notes_plane, notes_scales)
+        idx3 = load_list(offs3, "idx3")
+        idx2 = load_list(offs2, "idx2")
+        idx5 = load_list(offs5, "idx5")
+        lam_col = sb.tile([P, 1], F32)
+        nc.sync.dma_start(out=lam_col[:], in_=lam)
+        idx6 = load_list(offs6, "idx6")
+
+        query_bf = sb.tile([P, Q, PACK], BF16, align_bytes=64)
+        nc.vector.tensor_copy(
+            out=query_bf[:].rearrange("p (c i) t -> p c t i", i=4),
+            in_=query_rows[:].rearrange("p t (c i) -> p c t i", i=4),
+        )
+        query_codes = sb.tile([P, Q], U32, align_bytes=64)
+        query_plane = sb.tile([P, Q], U8, align_bytes=64)
+        nc.vector.quantize_mx(
+            out=query_codes[:].bitcast(FP8X4), scales=query_plane[:], in_=query_bf[:].rearrange("p q t -> p (q t)")
+        )
+
+        def score(bank, codes, plane):
+            nc.tensor.matmul_mx(
+                out=bank, lhsT=query_codes[:].bitcast(FP8X4), lhsT_scale=query_plane[:],
+                rhs=codes, rhs_scale=plane, start=True, stop=True,
+            )
+
+        a = sb.tile([P, POOL], F32)
+        for piece in range(POOL // PIECE):
+            lo, hi = piece * PIECE, (piece + 1) * PIECE
+            a_bank = psum.tile([P, PIECE], F32, name="a_bank%d" % piece)
+            score(a_bank[:], keys_codes[:, 2 * lo : 2 * hi].bitcast(FP4X4), keys_plane[:, lo:hi])
+            if piece % 2 == 0:
+                nc.vector.tensor_copy(out=a[:, lo:hi], in_=a_bank[:])
+            else:
+                nc.scalar.activation(a[:, lo:hi], a_bank[:], COPY)
+
+        a_picked = sb.tile([P, SLOTS], F32, tag="picked")
+        nc.vector.tensor_copy(slots(a_picked, 0), a[:].indirect(half(idx, 0)))
+        nc.scalar.activation(slots(a_picked, 1), a[:].indirect(half(idx, 1)), COPY)
+        nc.vector.tensor_copy(f1[:].indirect(idx4[:]), a_picked[:])
+
+        c0 = sb.tile([P, POOL], F32)
+        b = sb.tile([P, POOL], F32, tag="b")
+        c0_banks = []
+        b_banks = []
+        for n in range(POOL // BANK):
+            lo, hi = n * BANK, (n + 1) * BANK
+            c0_bank = psum.tile([P, BANK], F32, name="c0_bank%d" % n)
+            score(c0_bank[:], users_codes[:, 2 * lo : 2 * hi].bitcast(FP4X4), users_plane[:, lo:hi])
+            nc.scalar.activation(c0[:, lo:hi], c0_bank[:], COPY)
+            c0_banks.append(c0_bank)
+        c0_neg = sb.tile([P, SLOTS], F32)
+        nc.scalar.activation(c0_neg[:], c0[:].indirect(idx3[:]), COPY, scale=-1.0)
+        for n in range(POOL // BANK):
+            lo, hi = n * BANK, (n + 1) * BANK
+            b_bank = psum.tile([P, BANK], F32, name="b_bank%d" % n)
+            score(b_bank[:], notes_codes[:, lo:hi].bitcast(FP8X4), notes_plane[:, lo:hi])
+            nc.scalar.activation(b[:, lo:hi], b_bank[:], COPY)
+            b_banks.append(b_bank)
+        b_picked = sb.tile([P, SLOTS], F32)
+        nc.scalar.activation(b_picked[:], b[:].indirect(idx2[:]), COPY)
+
+        cc = sb.tile([P, POOL], F32, tag="cc")
+        for n in range(POOL // BANK):
+            lo, hi = n * BANK, (n + 1) * BANK
+            nc.vector.tensor_tensor(cc[:, lo:hi], c0_banks[n][:], f1[:, lo:hi], ALU.add)
+
+        w_neg = sb.tile([P, SLOTS], F32, tag="picked")
+        nc.vector.scalar_tensor_tensor(w_neg[:], b_picked[:], -1.0, c0_neg[:], ALU.mult, ALU.min)
+        cc_picked = sb.tile([P, SLOTS], F32, tag="b")
+        for h in range(2):
+            nc.scalar.activation(slots(cc_picked, h), cc[:].indirect(half(idx3, h)), COPY)
+        for h in range(2):
+            nc.vector.tensor_tensor(f2[:].indirect(half(idx5, h)), slots(cc_picked, h), slots(w_neg, h), ALU.add)
+
+        a_last = sb.tile([P, SLOTS], F32, tag="cc")
+        nc.scalar.activation(a_last[:], a[:].indirect(idx6[:]), COPY)
+
+        bb = sb.tile([P, POOL], F32)
+        for n in range(POOL // BANK):
+            lo, hi = n * BANK, (n + 1) * BANK
+            nc.vector.scalar_tensor_tensor(bb[:, lo:hi], f2[:, lo:hi], lam_col[:], b_banks[n][:], ALU.mult, ALU.add)
+
+        bb_picked = sb.tile([P, SLOTS], F32)
+        result = sb.tile([P, SLOTS], F32)
+        nc.vector.tensor_copy(slots(bb_picked, 0), bb[:].indirect(half(idx2, 0)))
+        nc.scalar.activation(slots(bb_picked, 1), bb[:].indirect(half(idx2, 1)), COPY)
+        for h, queue in ((1, nc.scalar), (0, nc.sync)):
+            nc.vector.tensor_tensor(slots(result, h), slots(bb_picked, h), slots(a_last, h), ALU.min)
+            queue.dma_start(out=slots(out, h), in_=slots(result, h))

@@ -20,7 +20,7 @@ POOL = 1024
 SLOTS = 512
 HALF = SLOTS // 2
 BANK = 512
-PIECE = 256
+GPSIMD_COLS = 320
 LIST_COLS = SLOTS // 16
 FLOPS = 2 * 512 * Q * 3 * POOL
 
@@ -57,12 +57,10 @@ def tile_attend_goaround_three_kernel(
         keys_plane = sb.tile([P, POOL], U8, align_bytes=64)
         users_plane = sb.tile([P, POOL], U8, align_bytes=64)
         notes_plane = sb.tile([P, POOL], U8, align_bytes=64)
-        f1 = sb.tile([P, POOL], F32)
         f2 = sb.tile([P, POOL], F32)
         nc.vector.memset(keys_plane[:].bitcast(I32), 0)
         nc.vector.memset(users_plane[:].bitcast(I32), 0)
         nc.vector.memset(notes_plane[:].bitcast(I32), 0)
-        nc.vector.memset(f1[:], 0.0)
         nc.vector.memset(f2[:], 0.0)
 
         query_rows = sb.tile([P, PACK, Q], F32)
@@ -75,7 +73,7 @@ def tile_attend_goaround_three_kernel(
         users_codes = sb.tile([P, 2 * POOL], U8, align_bytes=64)
         nc.sync.dma_start(out=users_codes[:].bitcast(I32), in_=users_words[0].bitcast(I32))
         load_scales(nc.sync, users_plane, users_scales)
-        notes_codes = sb.tile([P, POOL], U32, align_bytes=64)
+        notes_codes = sb.tile([P, POOL], U32, align_bytes=64, tag="notes")
         nc.sync.dma_start(
             out=notes_codes[:].bitcast(I32), in_=notes_words[0].rearrange("p n t -> p (n t)").bitcast(I32)
         )
@@ -87,7 +85,7 @@ def tile_attend_goaround_three_kernel(
         nc.sync.dma_start(out=lam_col[:], in_=lam)
         idx6 = load_list(offs6, "idx6")
 
-        query_bf = sb.tile([P, Q, PACK], BF16, align_bytes=64)
+        query_bf = sb.tile([P, Q, PACK], BF16, align_bytes=64, tag="f1")
         nc.vector.tensor_copy(
             out=query_bf[:].rearrange("p (c i) t -> p c t i", i=4),
             in_=query_rows[:].rearrange("p t (c i) -> p c t i", i=4),
@@ -98,6 +96,9 @@ def tile_attend_goaround_three_kernel(
             out=query_codes[:].bitcast(FP8X4), scales=query_plane[:], in_=query_bf[:].rearrange("p q t -> p (q t)")
         )
 
+        f1 = sb.tile([P, POOL], F32, align_bytes=64, tag="f1")
+        nc.vector.memset(f1[:], 0.0)
+
         def score(bank, codes, plane):
             nc.tensor.matmul_mx(
                 out=bank, lhsT=query_codes[:].bitcast(FP8X4), lhsT_scale=query_plane[:],
@@ -105,14 +106,16 @@ def tile_attend_goaround_three_kernel(
             )
 
         a = sb.tile([P, POOL], F32)
-        for piece in range(POOL // PIECE):
-            lo, hi = piece * PIECE, (piece + 1) * PIECE
-            a_bank = psum.tile([P, PIECE], F32, name="a_bank%d" % piece)
+        lo = 0
+        for piece, (width, on_vector) in enumerate(((512, False), (256, True), (128, True), (128, False))):
+            hi = lo + width
+            a_bank = psum.tile([P, width], F32, name="a_bank%d" % piece)
             score(a_bank[:], keys_codes[:, 2 * lo : 2 * hi].bitcast(FP4X4), keys_plane[:, lo:hi])
-            if piece % 2 == 0:
+            if on_vector:
                 nc.vector.tensor_copy(out=a[:, lo:hi], in_=a_bank[:])
             else:
                 nc.scalar.activation(a[:, lo:hi], a_bank[:], COPY)
+            lo = hi
 
         a_picked = sb.tile([P, SLOTS], F32, tag="picked")
         nc.vector.tensor_copy(slots(a_picked, 0), a[:].indirect(half(idx, 0)))
@@ -129,24 +132,27 @@ def tile_attend_goaround_three_kernel(
             score(c0_bank[:], users_codes[:, 2 * lo : 2 * hi].bitcast(FP4X4), users_plane[:, lo:hi])
             nc.scalar.activation(c0[:, lo:hi], c0_bank[:], COPY)
             c0_banks.append(c0_bank)
-        c0_neg = sb.tile([P, SLOTS], F32)
-        nc.scalar.activation(c0_neg[:], c0[:].indirect(idx3[:]), COPY, scale=-1.0)
         for n in range(POOL // BANK):
             lo, hi = n * BANK, (n + 1) * BANK
             b_bank = psum.tile([P, BANK], F32, name="b_bank%d" % n)
             score(b_bank[:], notes_codes[:, lo:hi].bitcast(FP8X4), notes_plane[:, lo:hi])
             nc.scalar.activation(b[:, lo:hi], b_bank[:], COPY)
             b_banks.append(b_bank)
+        c0_neg = sb.tile([P, SLOTS], F32, align_bytes=64, tag="notes")
+        nc.scalar.activation(c0_neg[:], c0[:].indirect(idx3[:]), COPY, scale=-1.0)
         b_picked = sb.tile([P, SLOTS], F32)
         nc.scalar.activation(b_picked[:], b[:].indirect(idx2[:]), COPY)
 
         cc = sb.tile([P, POOL], F32, tag="cc")
+        split = POOL - GPSIMD_COLS
+        nc.gpsimd.tensor_tensor(cc[:, split:], c0[:, split:], f1[:, split:], ALU.add)
         for n in range(POOL // BANK):
-            lo, hi = n * BANK, (n + 1) * BANK
-            nc.vector.tensor_tensor(cc[:, lo:hi], c0_banks[n][:], f1[:, lo:hi], ALU.add)
+            lo, hi = n * BANK, min((n + 1) * BANK, split)
+            nc.vector.tensor_tensor(cc[:, lo:hi], c0_banks[n][:, : hi - lo], f1[:, lo:hi], ALU.add)
 
         w_neg = sb.tile([P, SLOTS], F32, tag="picked")
-        nc.vector.scalar_tensor_tensor(w_neg[:], b_picked[:], -1.0, c0_neg[:], ALU.mult, ALU.min)
+        for h in range(2):
+            nc.vector.scalar_tensor_tensor(slots(w_neg, h), slots(b_picked, h), -1.0, slots(c0_neg, h), ALU.mult, ALU.min)
         cc_picked = sb.tile([P, SLOTS], F32, tag="b")
         for h in range(2):
             nc.scalar.activation(slots(cc_picked, h), cc[:].indirect(half(idx3, h)), COPY)

@@ -25,8 +25,8 @@ LIST_COLS = SLOTS // 16
 FLOPS = 2 * 512 * Q * 3 * POOL
 
 
-def load_scales(queue, plane, scales):
-    for quad in range(4):
+def load_scales(queues, plane, scales):
+    for quad, queue in enumerate(queues):
         queue.dma_start(
             out=plane[32 * quad : 32 * quad + 4, :].bitcast(I32),
             in_=scales[0, 4 * quad : 4 * quad + 4, :].bitcast(I32),
@@ -59,25 +59,25 @@ def tile_attend_goaround_three_kernel(
         notes_plane = sb.tile([P, POOL], U8, align_bytes=64)
         f2 = sb.tile([P, POOL], F32)
         nc.vector.memset(keys_plane[:].bitcast(I32), 0)
-        nc.vector.memset(users_plane[:].bitcast(I32), 0)
         nc.vector.memset(notes_plane[:].bitcast(I32), 0)
+        nc.vector.memset(users_plane[:].bitcast(I32), 0)
         nc.vector.memset(f2[:], 0.0)
 
         query_rows = sb.tile([P, PACK, Q], F32)
         nc.sync.dma_start(out=query_rows[:], in_=query.rearrange("(p j) q -> p j q", j=PACK))
         keys_codes = sb.tile([P, 2 * POOL], U8, align_bytes=64)
         nc.sync.dma_start(out=keys_codes[:].bitcast(I32), in_=keys_words[0].bitcast(I32))
-        load_scales(nc.scalar, keys_plane, keys_scales)
+        load_scales([nc.scalar, nc.scalar, nc.sync, nc.sync], keys_plane, keys_scales)
         idx = load_list(offs, "idx")
         idx4 = load_list(offs4, "idx4")
         users_codes = sb.tile([P, 2 * POOL], U8, align_bytes=64)
         nc.sync.dma_start(out=users_codes[:].bitcast(I32), in_=users_words[0].bitcast(I32))
-        load_scales(nc.sync, users_plane, users_scales)
+        load_scales([nc.sync] * 4, users_plane, users_scales)
         notes_codes = sb.tile([P, POOL], U32, align_bytes=64, tag="notes")
         nc.sync.dma_start(
             out=notes_codes[:].bitcast(I32), in_=notes_words[0].rearrange("p n t -> p (n t)").bitcast(I32)
         )
-        load_scales(nc.sync, notes_plane, notes_scales)
+        load_scales([nc.sync, nc.sync, nc.gpsimd, nc.gpsimd], notes_plane, notes_scales)
         idx3 = load_list(offs3, "idx3")
         idx2 = load_list(offs2, "idx2")
         idx5 = load_list(offs5, "idx5")
@@ -86,18 +86,22 @@ def tile_attend_goaround_three_kernel(
         idx6 = load_list(offs6, "idx6")
 
         query_bf = sb.tile([P, Q, PACK], BF16, align_bytes=64, tag="f1")
-        nc.vector.tensor_copy(
-            out=query_bf[:].rearrange("p (c i) t -> p c t i", i=4),
-            in_=query_rows[:].rearrange("p t (c i) -> p c t i", i=4),
-        )
         query_codes = sb.tile([P, Q], U32, align_bytes=64)
         query_plane = sb.tile([P, Q], U8, align_bytes=64)
-        nc.vector.quantize_mx(
-            out=query_codes[:].bitcast(FP8X4), scales=query_plane[:], in_=query_bf[:].rearrange("p q t -> p (q t)")
-        )
+        for lo in (0, Q // 2):
+            nc.vector.tensor_copy(
+                out=query_bf[:, lo : lo + Q // 2, :].rearrange("p (c i) t -> p c t i", i=4),
+                in_=query_rows[:, :, lo : lo + Q // 2].rearrange("p t (c i) -> p c t i", i=4),
+            )
+        for lo in (0, Q // 2):
+            nc.vector.quantize_mx(
+                out=query_codes[:, lo : lo + Q // 2].bitcast(FP8X4),
+                scales=query_plane[:, lo : lo + Q // 2],
+                in_=query_bf[:, lo : lo + Q // 2, :].rearrange("p q t -> p (q t)"),
+            )
 
         f1 = sb.tile([P, POOL], F32, align_bytes=64, tag="f1")
-        nc.vector.memset(f1[:], 0.0)
+        nc.gpsimd.memset(f1[:], 0.0)
 
         def score(bank, codes, plane):
             nc.tensor.matmul_mx(
@@ -122,8 +126,8 @@ def tile_attend_goaround_three_kernel(
         nc.scalar.activation(slots(a_picked, 1), a[:].indirect(half(idx, 1)), COPY)
         nc.vector.tensor_copy(f1[:].indirect(idx4[:]), a_picked[:])
 
-        c0 = sb.tile([P, POOL], F32)
-        b = sb.tile([P, POOL], F32, tag="b")
+        c0 = sb.tile([P, POOL], F32, tag="c0")
+        b = sb.tile([P, POOL], F32)
         c0_banks = []
         b_banks = []
         for n in range(POOL // BANK):
@@ -153,7 +157,7 @@ def tile_attend_goaround_three_kernel(
         w_neg = sb.tile([P, SLOTS], F32, tag="picked")
         for h in range(2):
             nc.vector.scalar_tensor_tensor(slots(w_neg, h), slots(b_picked, h), -1.0, slots(c0_neg, h), ALU.mult, ALU.min)
-        cc_picked = sb.tile([P, SLOTS], F32, tag="b")
+        cc_picked = sb.tile([P, SLOTS], F32, tag="c0")
         for h in range(2):
             nc.scalar.activation(slots(cc_picked, h), cc[:].indirect(half(idx3, h)), COPY)
         for h in range(2):

from contextlib import ExitStack

import concourse.mybir as mybir

F32 = mybir.dt.float32
BF16 = mybir.dt.bfloat16
I32 = mybir.dt.int32
U32 = mybir.dt.uint32
U16 = mybir.dt.uint16
U8 = mybir.dt.uint8
FP8X4 = mybir.dt.float8_e4m3fn_x4
FP4X4 = mybir.dt.float4_e2m1fn_x4
ALU = mybir.AluOpType
COPY = mybir.ActivationFunctionType.Copy

P = 128
PACK = 4
Q = 128
POOL = 1024
SLOTS = 512
HALF = SLOTS // 2
BANK = 512
GPSIMD_COLS = 320
LIST_COLS = SLOTS // 16
FLOPS = 2 * 512 * Q * 3 * POOL


def load_scales(queues, plane, scales):
    for quad, queue in enumerate(queues):
        queue.dma_start(
            out=plane[32 * quad : 32 * quad + 4, :].bitcast(I32),
            in_=scales[0, 4 * quad : 4 * quad + 4, :].bitcast(I32),
        )


def tile_attend_goaround_three_kernel(
    tc, query, keys_words, keys_scales, notes_words, notes_scales, users_words, users_scales,
    lam, offs, offs2, offs3, offs4, offs5, offs6, out,
):
    nc = tc.nc
    with ExitStack() as ctx:
        lists = ctx.enter_context(tc.tile_pool(name="lists", bufs=1))
        sb = ctx.enter_context(tc.tile_pool(name="sb", bufs=1))
        psum = ctx.enter_context(tc.psum_pool(name="psum", bufs=1))

        def load_list(source, name):
            held = lists.tile([P, LIST_COLS], U16, name=name)
            nc.sync.dma_start(held[:], source)
            return held

        def half(held, h):
            return held[:, h * (LIST_COLS // 2) : (h + 1) * (LIST_COLS // 2)]

        def slots(values, h):
            return values[:, h * HALF : (h + 1) * HALF]

        keys_plane = sb.tile([P, POOL], U8, align_bytes=64)
        users_plane = sb.tile([P, POOL], U8, align_bytes=64)
        notes_plane = sb.tile([P, POOL], U8, align_bytes=64)
        f2 = sb.tile([P, POOL], F32)
        nc.vector.memset(keys_plane[:].bitcast(I32), 0)
        nc.vector.memset(notes_plane[:].bitcast(I32), 0)
        nc.vector.memset(users_plane[:].bitcast(I32), 0)
        nc.vector.memset(f2[:], 0.0)

        query_rows = sb.tile([P, PACK, Q], F32)
        nc.sync.dma_start(out=query_rows[:], in_=query.rearrange("(p j) q -> p j q", j=PACK))
        keys_codes = sb.tile([P, 2 * POOL], U8, align_bytes=64)
        nc.sync.dma_start(out=keys_codes[:].bitcast(I32), in_=keys_words[0].bitcast(I32))
        load_scales([nc.scalar, nc.scalar, nc.sync, nc.sync], keys_plane, keys_scales)
        idx = load_list(offs, "idx")
        idx4 = load_list(offs4, "idx4")
        users_codes = sb.tile([P, 2 * POOL], U8, align_bytes=64)
        nc.sync.dma_start(out=users_codes[:].bitcast(I32), in_=users_words[0].bitcast(I32))
        load_scales([nc.sync] * 4, users_plane, users_scales)
        notes_codes = sb.tile([P, POOL], U32, align_bytes=64, tag="notes")
        nc.sync.dma_start(
            out=notes_codes[:].bitcast(I32), in_=notes_words[0].rearrange("p n t -> p (n t)").bitcast(I32)
        )
        load_scales([nc.sync, nc.sync, nc.gpsimd, nc.gpsimd], notes_plane, notes_scales)
        idx3 = load_list(offs3, "idx3")
        idx2 = load_list(offs2, "idx2")
        idx5 = load_list(offs5, "idx5")
        lam_col = sb.tile([P, 1], F32)
        nc.sync.dma_start(out=lam_col[:], in_=lam)
        idx6 = load_list(offs6, "idx6")

        query_bf = sb.tile([P, Q, PACK], BF16, align_bytes=64, tag="f1")
        query_codes = sb.tile([P, Q], U32, align_bytes=64)
        query_plane = sb.tile([P, Q], U8, align_bytes=64)
        for lo in (0, Q // 2):
            nc.vector.tensor_copy(
                out=query_bf[:, lo : lo + Q // 2, :].rearrange("p (c i) t -> p c t i", i=4),
                in_=query_rows[:, :, lo : lo + Q // 2].rearrange("p t (c i) -> p c t i", i=4),
            )
        for lo in (0, Q // 2):
            nc.vector.quantize_mx(
                out=query_codes[:, lo : lo + Q // 2].bitcast(FP8X4),
                scales=query_plane[:, lo : lo + Q // 2],
                in_=query_bf[:, lo : lo + Q // 2, :].rearrange("p q t -> p (q t)"),
            )

        f1 = sb.tile([P, POOL], F32, align_bytes=64, tag="f1")
        nc.gpsimd.memset(f1[:], 0.0)

        def score(bank, codes, plane):
            nc.tensor.matmul_mx(
                out=bank, lhsT=query_codes[:].bitcast(FP8X4), lhsT_scale=query_plane[:],
                rhs=codes, rhs_scale=plane, start=True, stop=True,
            )

        a = sb.tile([P, POOL], F32)
        lo = 0
        for piece, (width, on_vector) in enumerate(((512, False), (256, True), (128, True), (128, False))):
            hi = lo + width
            a_bank = psum.tile([P, width], F32, name="a_bank%d" % piece)
            score(a_bank[:], keys_codes[:, 2 * lo : 2 * hi].bitcast(FP4X4), keys_plane[:, lo:hi])
            if on_vector:
                nc.vector.tensor_copy(out=a[:, lo:hi], in_=a_bank[:])
            else:
                nc.scalar.activation(a[:, lo:hi], a_bank[:], COPY)
            lo = hi

        a_picked = sb.tile([P, SLOTS], F32, tag="picked")
        nc.vector.tensor_copy(slots(a_picked, 0), a[:].indirect(half(idx, 0)))
        nc.scalar.activation(slots(a_picked, 1), a[:].indirect(half(idx, 1)), COPY)
        nc.vector.tensor_copy(f1[:].indirect(idx4[:]), a_picked[:])

        c0 = sb.tile([P, POOL], F32, tag="c0")
        b = sb.tile([P, POOL], F32)
        c0_banks = []
        b_banks = []
        for n in range(POOL // BANK):
            lo, hi = n * BANK, (n + 1) * BANK
            c0_bank = psum.tile([P, BANK], F32, name="c0_bank%d" % n)
            score(c0_bank[:], users_codes[:, 2 * lo : 2 * hi].bitcast(FP4X4), users_plane[:, lo:hi])
            nc.scalar.activation(c0[:, lo:hi], c0_bank[:], COPY)
            c0_banks.append(c0_bank)
        for n in range(POOL // BANK):
            lo, hi = n * BANK, (n + 1) * BANK
            b_bank = psum.tile([P, BANK], F32, name="b_bank%d" % n)
            score(b_bank[:], notes_codes[:, lo:hi].bitcast(FP8X4), notes_plane[:, lo:hi])
            nc.scalar.activation(b[:, lo:hi], b_bank[:], COPY)
            b_banks.append(b_bank)
        c0_neg = sb.tile([P, SLOTS], F32, align_bytes=64, tag="notes")
        nc.scalar.activation(c0_neg[:], c0[:].indirect(idx3[:]), COPY, scale=-1.0)
        b_picked = sb.tile([P, SLOTS], F32)
        nc.scalar.activation(b_picked[:], b[:].indirect(idx2[:]), COPY)

        cc = sb.tile([P, POOL], F32, tag="cc")
        split = POOL - GPSIMD_COLS
        nc.gpsimd.tensor_tensor(cc[:, split:], c0[:, split:], f1[:, split:], ALU.add)
        for n in range(POOL // BANK):
            lo, hi = n * BANK, min((n + 1) * BANK, split)
            nc.vector.tensor_tensor(cc[:, lo:hi], c0_banks[n][:, : hi - lo], f1[:, lo:hi], ALU.add)

        w_neg = sb.tile([P, SLOTS], F32, tag="picked")
        for h in range(2):
            nc.vector.scalar_tensor_tensor(slots(w_neg, h), slots(b_picked, h), -1.0, slots(c0_neg, h), ALU.mult, ALU.min)
        cc_picked = sb.tile([P, SLOTS], F32, tag="c0")
        for h in range(2):
            nc.scalar.activation(slots(cc_picked, h), cc[:].indirect(half(idx3, h)), COPY)
        for h in range(2):
            nc.vector.tensor_tensor(f2[:].indirect(half(idx5, h)), slots(cc_picked, h), slots(w_neg, h), ALU.add)

        a_last = sb.tile([P, SLOTS], F32, tag="cc")
        nc.scalar.activation(a_last[:], a[:].indirect(idx6[:]), COPY)

        bb = sb.tile([P, POOL], F32)
        for n in range(POOL // BANK):
            lo, hi = n * BANK, (n + 1) * BANK
            nc.vector.scalar_tensor_tensor(bb[:, lo:hi], f2[:, lo:hi], lam_col[:], b_banks[n][:], ALU.mult, ALU.add)

        bb_picked = sb.tile([P, SLOTS], F32)
        result = sb.tile([P, SLOTS], F32)
        nc.vector.tensor_copy(slots(bb_picked, 0), bb[:].indirect(half(idx2, 0)))
        nc.scalar.activation(slots(bb_picked, 1), bb[:].indirect(half(idx2, 1)), COPY)
        for h, queue in ((1, nc.scalar), (0, nc.sync)):
            nc.vector.tensor_tensor(slots(result, h), slots(bb_picked, h), slots(a_last, h), ALU.min)
            queue.dma_start(out=slots(out, h), in_=slots(result, h))
